import numpy as np, ml_dtypes
CORES = [10,34,74,98]
N = 4
BF = ml_dtypes.bfloat16
def gentries(a):
    return np.ascontiguousarray(a.reshape(8, 16, -1).transpose(0, 2, 1)).reshape(8, -1)
def gtable(e):
    e = np.asarray(e); return np.ascontiguousarray(e.reshape(8, -1, 16).transpose(0, 2, 1)).reshape(128, -1).astype(np.int32)
W, B, E, SH, L, H = 4096, 64, 64, 6, 6, 1
R = L * B
def parts(rng):
    Y = rng.integers(0, 256, (N, 8, 16, W)); X = rng.integers(0, 256, (N, 8, 16, R)); m = rng.integers(0, W, (N, 8, R))
    lev = np.arange(B, R) // B; h = []
    for k in range(2):
        at = np.where(rng.random((N, 8, R - B)) < 0.5, 0, (lev * rng.random((N, 8, R - B))).astype(np.int64))
        h.append(rng.integers(0, H + 1, (N, 8, R - B)) * R + at * B + rng.integers(0, B, (N, 8, R - B)))
    a, b = rng.integers(0, W, (N, 8, B)), rng.integers(0, W, (N, 8, B)); far = rng.random((N, 8, B)) < 0.7
    lo = np.where(far, rng.integers(0, W // 4, (N, 8, B)), np.minimum(a, b)); hi = np.where(far, rng.integers(3 * W // 4, W, (N, 8, B)), np.maximum(a, b))
    return Y, X, h[0], h[1], m, lo, hi
def pack(Y, X, a, b, m, lo, hi):
    return {"ytab": np.ascontiguousarray(Y.reshape(N, 128, W)).astype(np.float32).astype(BF), "xrow": np.ascontiguousarray(X.reshape(N, 128, R)).astype(np.float32).astype(BF),
            "ha": np.stack([gtable(v) for v in a]), "hb": np.stack([gtable(v) for v in b]), "home": np.stack([gtable(v) for v in m]), "lo0": np.stack([gtable(v) for v in lo]), "hi0": np.stack([gtable(v) for v in hi])}
def setup_inputs(rng):
    return pack(*parts(rng))
def setup_inputs_ties(rng):
    Y, X, a, b, m, lo, hi = parts(rng)
    Y = np.take_along_axis(rng.integers(0, 256, (N, 8, 16, 4)), rng.integers(0, 4, (N, 8, 1, W)), 3)
    Y[:, 0] = Y[:, 0, :, :1]
    hi = np.where(rng.random(hi.shape) < 0.2, np.minimum(lo + rng.integers(0, E, hi.shape), W - 1), hi)
    m[:, :, :B] = (lo + hi) >> 1
    return pack(Y, X, a, b, m, lo, hi)
def setup_inputs_narrow(rng):
    Y, X, a, b, m, lo, hi = parts(rng)
    lo = rng.integers(0, W - 1, lo.shape); lo[:, :4] = rng.integers(0, W - 1024, (1, 4, 1)) + rng.integers(0, 40, (N, 4, B))
    hi = np.minimum(lo + rng.choice(np.array([0, 1, 2, E - 1, E, E + 1, 2 * E + 1, 300]), lo.shape), W - 1)
    for k, (p, q) in enumerate(((0, 0), (W - 1, W - 1), (0, W - 1), (W - 2, W - 1), (0, 1))): lo[:, 3:, k] = p; hi[:, 3:, k] = q
    t = rng.random((N, 5, R - B)) < 0.2
    a[:, 3:] = np.where(t, 1, a[:, 3:]); b[:, 3:] = np.where(t, H * R, b[:, 3:])
    lo[:, 7] = (E * np.arange(B)) % W; hi[:, 7] = np.minimum(lo[:, 7] + E, W - 1)
    o = np.arange(R - B); a[:, 7] = o; b[:, 7] = o + (o % B < B - 1)
    return pack(Y, X, a, b, m, lo, hi)
def setup_inputs_alike(rng):
    Y, X, a, b, m, lo, hi = parts(rng); lev = np.arange(B, R) // B
    v = a.reshape(N, 8, L - 1, B); a = np.where((np.arange(8) % 2 == 0)[None, :, None, None], v[..., :1], v).reshape(N, 8, R - B)
    a[:, 4] = rng.integers(0, H + 1, (N, 1)) * R + rng.integers(0, B, (N, 1))
    b[:, 1] = np.where(rng.random((N, R - B)) < 0.5, a[:, 1], b[:, 1]); b[:, 2] = a[:, 2]
    a[:, 3] = a[:, 3] % R; b[:, 3] = b[:, 3] % R
    a[:, 5] = a[:, 5] % R + H * R; b[:, 5] = b[:, 5] % R + H * R
    for w in (a, b): w[:, 7] = rng.integers(0, H + 1, (N, R - B)) * R + np.where(rng.random((N, R - B)) < 0.5, 0, B * lev - 1)
    return pack(Y, X, a, b, m, lo, hi)
def setup_inputs_far(rng):
    Y, X, a, b, m, lo, hi = parts(rng)
    Y = 255 * rng.integers(0, 2, Y.shape); X = 255 * rng.integers(0, 2, (N, 8, 1, R)) + np.zeros((1, 1, 16, 1), np.int64); m = (W - 1) * rng.integers(0, 2, m.shape)
    Y[:, 0] = 255; X[:, 0] = 0; Y[:, 1] = 0; X[:, 1] = 255; lo[:, :, :8] = 0; m[:, :, :4] = W - 1; m[:, :, 4:8] = 0
    for i, p, q, c in ((8, W - 1, W - 1, 0), (12, W - 16, W - 1, 0), (16, 0, 31, W - 1), (20, 1, 15, W - 1)): lo[:, :2, i:i + 4] = p; hi[:, :2, i:i + 4] = q; m[:, :2, i:i + 4] = c
    a[:, 1, ::B] = 8; b[:, 1, ::B] = H * R + 9
    Y[:, 2] = rng.integers(0, 2, (N, 16, W)); X[:, 2] = 255; hi[:, 2] = np.minimum(lo[:, 2] + 2 * E, W - 1)
    return pack(Y, X, a, b, m, lo, hi)
def setup_inputs_spread(rng):
    Y, X, a, b, m, lo, hi = parts(rng); lev = np.arange(B, R) // B
    Y = (np.exp2(rng.integers(1, 9, (N, 8, 1, W))) * rng.random(Y.shape)).astype(np.int64); X = (np.exp2(rng.integers(1, 9, (N, 8, 1, R))) * rng.random(X.shape)).astype(np.int64)
    a = (a // R) * R + (B * lev * rng.random(a.shape) ** 3).astype(np.int64); m = (W * rng.random(m.shape) ** 2).astype(np.int64)
    return pack(Y, X, a, b, m, lo, hi)
def check_inputs(d):
    bad = []
    for k in ("ytab", "xrow"):
        v = np.asarray(d[k]).astype(np.float32)
        if not np.all((v >= 0) & (v <= 255) & (v == np.floor(v))): bad.append("whole numbers of " + k)
    for k in ("home", "lo0", "hi0"):
        if np.min(d[k]) < 0 or np.max(d[k]) >= W: bad.append("range of " + k)
    if np.any(d["lo0"] > d["hi0"]): bad.append("lo0 over hi0")
    lev = np.arange(B, R) // B
    for k in ("ha", "hb"):
        h = np.stack([gentries(v) for v in d[k]]).astype(np.int64)
        if np.min(h) < 0 or np.max(h) >= (H + 1) * R or np.any(h % R >= B * lev): bad.append("rows that " + k + " names")
    return bad
def reference(ytab, xrow, ha, hb, home, lo0, hi0):
    Y = ytab.astype(np.float32).astype(np.int32).reshape(N, 8, 16, W); X = xrow.astype(np.float32).astype(np.int32).reshape(N, 8, 16, R)
    a, b, m, first, last = [np.stack([gentries(v) for v in t]).astype(np.int64) for t in (ha, hb, home, lo0, hi0)]
    e = np.arange(E); wins = []
    for ps in range(2):
        arg = np.zeros((N, 8, R), np.int64)
        for l in range(L):
            s = l * B
            if l == 0: lo, hi = first, last
            else:
                known = np.concatenate([np.roll(arg, -k, axis=0) for k in range(H + 1)], axis=2)
                u = np.take_along_axis(known, a[:, :, s - B:s], 2); v = np.take_along_axis(known, b[:, :, s - B:s], 2)
                lo, hi = np.minimum(u, v), np.maximum(u, v)
            j = lo[..., None] + (((hi - lo)[..., None] * e) >> SH)
            y = np.take_along_axis(Y, j.reshape(N, 8, 1, B * E), 3).reshape(N, 8, 16, B, E)
            cost = np.add.reduce(np.abs(X[..., s:s + B, None] - y), axis=2) + (np.abs(j - m[:, :, s:s + B, None]) >> 4)
            k = np.argmin(cost, axis=3)
            arg[:, :, s:s + B] = np.take_along_axis(j, k[..., None], 3)[..., 0]
        X = np.abs(X - np.take_along_axis(Y, arg[:, :, None, :], 3))
        wins.append(arg)
    both = np.concatenate(wins, axis=2)
    return {"argm": np.stack([gtable(v) for v in both]).astype(np.float32), "xo": X.reshape(N, 128, R).astype(np.float32)}

import numpy as np
from concourse.mybir import AluOpType, AxisListType, ActivationFunctionType

A = AluOpType
F = ActivationFunctionType
L, R, NI = 6, 384, 4096
BIG = float(2 ** 22)
CJ = 2048.0 - 63.0 / 128.0
SBL = [0, 2]
SPLIT = [([0], [1]), ([2], [3])]
CFG = {(p, l): (SPLIT, [[0], [1]]) for p in range(2) for l in range(L)}
CH = 256
COST = dict(GE=1.5e-3, CY=0.83e-3, WAKE=0.12, REMOTE=4.0, PE=0.5e-3, FIX=0.01, YT=7.0)
PRI = dict(chain=1.0, relu=2.0, p1=1.5, xup=3.0)

SCRATCH = {
    "yt": ("sbuf", [128, NI], "bfloat16"),
    "x0": ("sbuf", [128, R], "bfloat16"), "x1": ("sbuf", [128, R], "bfloat16"), "xf": ("sbuf", [128, R], "float32"),
    "rep0": ("sbuf", [128, L * 2 * CH], "bfloat16"), "rep1": ("sbuf", [128, L * 2 * CH], "bfloat16"),
    "am": ("sbuf", [128, 48], "float32"), "wall": ("sbuf", [128, 48], "int32"),
    "hm": ("sbuf", [128, 24], "int32"), "hf": ("sbuf", [128, 24], "float32"),
    "lh": ("sbuf", [128, 8], "int32"), "lob": ("sbuf", [128, 8], "float32"),
    "hi40": ("sbuf", [128, 40], "int32"), "h1": ("sbuf", [128, 40], "int32"), "h2": ("sbuf", [128, 40], "int32"),
    "h3": ("sbuf", [128, 40], "int32"), "h4": ("sbuf", [128, 40], "int32"), "h5": ("sbuf", [128, 40], "int32"),
    "h6": ("sbuf", [128, 40], "int32"), "hl": ("sbuf", [128, 40], "uint16"), "hs": ("sbuf", [128, 20], "uint16"),
    "ones": ("sbuf", [128, 128], "float32"), "bo1": ("sbuf", [128, 128], "float32"), "bo": ("sbuf", [128, 128], "float32"),
    "idm": ("sbuf", [128, 128], "float32"), "etab": ("sbuf", [128, 64], "float32"), "e0": ("sbuf", [128, 128], "float32"),
    "idb": ("sbuf", [128, 128], "bfloat16"), "i64": ("sbuf", [128, 128], "float16"),
    "m1": ("sbuf", [128, 64], "float32"), "m2": ("sbuf", [128, 32], "float32"),
    "mk": ("sbuf", [128, 64], "float32"), "mks": ("sbuf", [128, 128], "float32"),
    "col": ("sbuf", [128, 8], "float32"), "qt": ("sbuf", [128, 512], "float32"), "qw": ("sbuf", [128, 512], "float16"),
    "zs": ("sbuf", [128, 160], "bfloat16"), "zr": ("sbuf", [128, 160], "bfloat16"), "zd": ("sbuf", [128, 160], "bfloat16"),
    "bos": ("sbuf", [128, 128], "float16"), "seg": ("sbuf", [128, 64], "float32"), "nst": ("sbuf", [128, 128], "float32"),
    "cli": ("sbuf", [128, 4], "int32"), "clist": ("sbuf", [128, 4], "uint16"),
    "dg0": ("sbuf", [128, 128], "float16"),
}
for _p in range(2):
    SCRATCH["win%d" % _p] = ("sbuf", [128, 2 * R], "float32")
    SCRATCH["as%d" % _p] = ("sbuf", [128, 32 * 64], "bfloat16")
    SCRATCH["dv%d" % _p] = ("sbuf", [128, 32 * 64], "bfloat16")
    SCRATCH["rv%d" % _p] = ("sbuf", [128, 32 * 64], "bfloat16")
    SCRATCH["ks%d" % _p] = ("sbuf", [128, 256], "float32")
    SCRATCH["ki%d" % _p] = ("sbuf", [128, 4], "int32")
    SCRATCH["ei%d" % _p] = ("sbuf", [128, 4], "int32")
    SCRATCH["tf%d" % _p] = ("sbuf", [128, 4], "float32")
    SCRATCH["wf%d" % _p] = ("sbuf", [128, 8], "float32")
    SCRATCH["wo%d" % _p] = ("sbuf", [128, 8], "uint16")
    SCRATCH["dg%d" % (_p + 1)] = ("sbuf", [128, 64], "float16")
    SCRATCH["dx%d" % _p] = ("sbuf", [128, 64], "bfloat16")
    SCRATCH["um%d" % _p] = ("sbuf", [128, 128], "float32")
    SCRATCH["us%d" % _p] = ("sbuf", [128, 128], "float32")
    SCRATCH["vz%d" % _p] = ("sbuf", [128, 32], "float32")
    SCRATCH["z%d" % _p] = ("sbuf", [128, 32], "float16")
    for _u in range(2): SCRATCH["K%d%d" % (_p, _u)] = ("psum", [128, 512], "float32")
    SCRATCH["Q%d" % _p] = ("psum", [128, 512], "float32")
    SCRATCH["KN%d" % _p] = ("psum", [128, 512], "float32")
for _s in range(3):
    SCRATCH["sc%d" % _s] = ("sbuf", [128, 24], "float32")
    SCRATCH["ofv%d" % _s] = ("sbuf", [128, 128], "uint16")
    SCRATCH["ofs%d" % _s] = ("sbuf", [128, 128], "uint16")
    SCRATCH["pa%d" % _s] = ("sbuf", [128, 256], "float32")
    SCRATCH["pn%d" % _s] = ("sbuf", [128, 256], "float16")

LOADS = ["lo", "hi", "x", "home", "y", "h"]
SEMAPHORES = (["cV", "cS", "cT", "cG", "snt", "st"] + ["ld_" + k for k in LOADS]
              + ["arr%d_%d" % (p, l) for p in range(2) for l in range(L - 1)])


def build(g, core, T, topo, rank):
    ops = []; ctx = [("setup", 0, 0, 0)]
    last_w, readers = {}, {}
    GE, CY, PE = COST["GE"], COST["CY"], COST["PE"]

    def add(q, dur, fn, r=(), w=(), n=1, sem=None, val=0, lat=0.0, grp=None):
        i = len(ops); deps = {}
        for t in r:
            if t in last_w: deps[last_w[t]] = "raw"
        for t in w:
            if t in last_w: deps.setdefault(last_w[t], "waw")
            for k in readers.get(t, ()):
                if k != i: deps.setdefault(k, "war")
        for t in r: readers.setdefault(t, []).append(i)
        for t in w: last_w[t] = i; readers[t] = []
        ops.append(dict(q=q, dur=dur, fn=fn, deps=deps, n=n, sem=sem, val=val, lat=lat, grp=grp, tag=ctx[0]))
        return i

    V, S, G, TE, SY = g.vector, g.scalar, g, g.tensor, g.sync
    sv = lambda n, c=1.0: COST["FIX"] + max(64, n * c) * CY

    def ts(out, in0, s1, s2, o0, o1, r, w, n, c=1.0):
        if o1 is None: add("V", sv(n, c), lambda: V.tensor_scalar(out, in0, s1, None, o0), r, w)
        else: add("V", sv(n, c), lambda: V.tensor_scalar(out, in0, s1, s2, o0, o1), r, w)
    def tt(out, a, b, op, r, w, n, c=2.0, gather=False):
        add("V", 0.05 + n * GE if gather else sv(n, c), lambda: V.tensor_tensor(out, a, b, op), r, w)
    def cp(out, in_, r, w, n, c=1.0, gather=False):
        add("V", 0.05 + n * GE if gather else sv(n, c), lambda: V.tensor_copy(out, in_), r, w)
    def ms(ap, v, w, n, r=()):
        add("V", sv(n), lambda: V.memset(ap, v), r, w)
    def scan(out, d0, d1, init, o0, o1, r, w, n):
        add("V", sv(n), lambda: V.tensor_tensor_scan(out, d0, d1, init, o0, o1), r, w)
    def act(out, in_, r, w, n, bias=0.0, scale=1.0, f=F.Abs):
        add("S", 0.065 + n * CY, lambda: S.activation(out, in_, f, bias=bias, scale=scale), r, w)

    def load(q, key, out, in_, tok, lat):
        eng = SY if q == "SY" else S
        add(q, 0.1, lambda: eng.dma_start(out, in_), (), (tok,), sem="ld_" + key, val=16, lat=lat)
    load("S", "lo", T.lh[:, 0:4], T.lo0[:], "lo", 1.8)
    load("SY", "hi", T.lh[:, 4:8], T.hi0[:], "hi", 1.8)
    load("S", "x", T.x0[:], T.xrow[:], "x0", 2.2)
    load("SY", "home", T.hm[:], T.home[:], "hm", 2.2)
    load("SY", "y", T.yt[:], T.ytab[:], "yt", COST["YT"])
    for l in range(L - 1):
        for k, (nm, q) in enumerate((("ha", "S"), ("hb", "SY"))):
            eng = SY if q == "SY" else S
            add(q, 0.1, lambda eng=eng, o=8 * l + 4 * k, t=T[nm][:, 4 * l:4 * l + 4]: eng.dma_start(T.hi40[:, o:o + 4], t), (), ("%s%d" % (nm, l),), sem="ld_h", val=32 * (L - 1), lat=7.5)
    HT = ["%s%d" % (nm, l) for l in range(L - 1) for nm in ("ha", "hb")]

    ms(T.ones[:], 1.0, ["ones"], 128)
    def aff(out, in_, pat, op, base, cm, r, w): add("G", 0.4, lambda: G.affine_select(out, in_, pat, op, 0.0, base, cm), r, w)
    add("G", 0.25, lambda: G.iota(T.etab[:], [[1, 64]], 0, 0, allow_small_or_imprecise_dtypes=True), (), ["etab"])
    aff(T.idm[:], T.ones[:], [[-1, 128]], A.is_equal, 0, 1, ["ones"], ["idm"])
    aff(T.bo1[:], T.ones[:], [[-16, 8], [0, 16]], A.is_ge, 0, 1, ["ones"], ["bo1"])
    aff(T.bo[:], T.bo1[:], [[16, 8], [0, 16]], A.is_ge, 15, -1, ["bo1"], ["bo"])
    add("G", 0.35, lambda: G.iota(T.e0[:], [[0, 8], [1, 16]], 0, 0, allow_small_or_imprecise_dtypes=True), (), ["e0"])
    add("G", 0.15, lambda: G.iota(T.cli[:], [[1, 4]], 0, 0), (), ["cli"])
    cp(T.clist[:], T.cli[:], ["cli"], ["clist"], 4)
    ms(T.seg[:], -1.0, ["seg0"], 64)
    ms(T.seg[:, 0:1], BIG, ["seg"], 1, ["seg0"])
    tt(T.m1[:], T.idm[:, 0:64], T.idm[:, 64:128], A.add, ["idm"], ["m1"], 64)
    tt(T.m2[:], T.m1[:, 0:32], T.m1[:, 32:64], A.add, ["m1"], ["m2"], 32)
    tt(T.mk[:, 0:16], T.m2[:, 0:16], T.m2[:, 16:32], A.add, ["m2"], ["mk16"], 16)
    cp(T.mk[:, 16:32], T.mk[:, 0:16], ["mk16"], ["mk32"], 16)
    cp(T.mk[:, 32:64], T.mk[:, 0:32], ["mk16", "mk32"], ["mk"], 32)
    add("V", sv(8), lambda: V.tensor_reduce(T.col[:, 0:1], T.mk[:, 1:16:2], AxisListType.X, A.add), ["mk16"], ["odd"])
    ts(T.col[:, 1:2], T.col[:, 0:1], 2.0, -1.0, A.mult, A.add, ["odd"], ["sgn"], 1)
    tt(T.col[:, 2:3], T.mk[:, 0:1], T.mk[:, 1:2], A.add, ["mk16"], ["ab"], 1)
    ts(T.col[:, 3:4], T.mk[:, 0:1], -64.0, None, A.mult, None, ["mk16"], ["a64_0"], 1)
    for c in range(1, 4):
        ts(T.col[:, 3 + c:4 + c], T.col[:, 2:3], 16.0 * c, T.col[:, 3:4], A.mult, A.add, ["ab", "a64_0"], ["a64_%d" % c], 1)
    for c in range(4):
        q = T.qt[:, 128 * c:128 * c + 128]
        act(q, T.e0[:], ["e0", "ab", "a64_%d" % c], ["qt%d" % c], 128, bias=T.col[:, 3 + c:4 + c], scale=T.col[:, 2:3], f=F.Identity)
        tt(T.qw[:, 128 * c:128 * c + 128], q, T.bo[:], A.mult, ["qt%d" % c, "bo"], ["qw%d" % c], 128)
    QWT = ["qw%d" % c for c in range(4)]
    ts(T.bos[:, 0:128:2], T.bo[:, 0:128:2], -1.0, None, A.mult, None, ["bo"], ["bosA"], 64)
    cp(T.bos[:, 1:128:2], T.bo[:, 1:128:2], ["bo"], ["bosB"], 64)
    act(T.idb[:], T.idm[:], ["idm"], ["idb"], 128, f=F.Identity)
    for nm, c in (("zs", 64.0), ("zr", 128.0), ("zd", -64.0)):
        ms(T[nm][:], 0.0, [nm + "0"], 160)
        act(T[nm][:, 15:143:16], T.bo[:, 0:128:16], ["bo", nm + "0"], [nm], 8, scale=c, f=F.Identity)
    ts(T.i64[:], T.idm[:], 64.0, None, A.mult, None, ["idm"], ["i64"], 128)
    ts(T.nst[:], T.e0[:], 0.0, None, A.is_gt, None, ["e0"], ["nst"], 128)
    for k in range(2):
        act(T.mks[:, 64 * k:64 * k + 64], T.mk[:], ["mk16", "mk32", "mk", "sgn"], ["mks%d" % k], 64, scale=T.col[:, 1:2], f=F.Identity)

    for k, nm in ((0, "lo"), (4, "hi")):
        ts(T.lob[:, k:k + 4], T.lh[:, k:k + 4], -2048.0, 1.0 / 64, A.add, A.mult, [nm], [nm + "b"], 4)
    cp(T.hf[:], T.hm[:], ["hm"], ["hf"], 24)
    ts(T.h1[:], T.hi40[:], 384.0, -384.0, A.is_ge, A.mult, HT, ["h1"], 40)
    tt(T.h2[:], T.hi40[:], T.h1[:], A.add, HT + ["h1"], ["h2"], 40)
    ts(T.h3[:], T.h2[:], 960, None, A.bitwise_and, None, ["h2"], ["h3"], 40)
    tt(T.h4[:], T.h2[:], T.h3[:], A.add, ["h2", "h3"], ["h4"], 40)
    ts(T.h5[:], T.h1[:], -1.0 / 6, None, A.mult, None, ["h1"], ["h5"], 40)
    tt(T.h6[:], T.h4[:], T.h5[:], A.add, ["h4", "h5"], ["h6"], 40)
    cp(T.hl[:], T.h6[:], ["h6"], ["hl"], 40)
    cp(T.hs[:], T.h6[:, 0:40:2], ["h6"], ["hs"], 20)

    def xtok(p, l, a): return "x0" if p == 0 else "x1.%d.%d" % (l, a)
    reptok = {}
    def reps(p, l, u):
        vb = CFG[p, l][0][u][1]; ctx[0] = ("reps", p, l, u)
        o = 2 * CH * l + CH * u; t = "rep%d.%d.%d" % (p, l, u)
        x = T["x%d" % p]; q = 1 - p; nb = len(vb); n = 16
        def mm():
            return [TE.matmul(T["Q%d" % q][:, k:k + n], T.idb[:], x[:, 64 * l + 16 * vb[k // n % nb]:64 * l + 16 * vb[k // n % nb] + n], True, True) for k in range(0, CH, n)]
        add("T", CH // n * 64 * PE, mm, ["idb"] + [xtok(p, l, a) for a in vb], ["Q%d" % q], n=CH // n)
        act(T["rep%d" % p][:, o:o + CH], T["Q%d" % q][:, 0:CH], ["Q%d" % q], [t], CH, f=F.Identity)
        reptok[p, l, u] = [t]

    def lists(p, s, l, lotok):
        sc = T["sc%d" % s]; t = "sc%d." % s
        lo, hi = (T.lob[:, 0:4], T.lob[:, 4:8]) if s == 2 else (sc[:, 0:4], sc[:, 4:8])
        tt(sc[:, 8:12], hi, lo, A.subtract, lotok, [t + "D"], 4)
        ts(sc[:, 12:16], lo, 64.0, CJ, A.mult, A.add, lotok, [t + "B1"], 4)
        tt(sc[:, 16:20], sc[:, 12:16], T.hf[:, 4 * l:4 * l + 4], A.subtract, [t + "B1", "hf"], [t + "B2"], 4)
        pa = T["pa%d" % s]; po = 0; vo = 0; pt = []
        for sb, vb in CFG[p, l][0]:
            nb = len(vb); o = po + 64 * len(sb)
            for k, a in enumerate(vb):
                ts(T["ofv%d" % s][:, vo + k:vo + 64 * nb:nb], T.etab[:], sc[:, 8 + a:9 + a], sc[:, 12 + a:13 + a], A.mult, A.add, ["etab", t + "D", t + "B1"], ["ofv%d.%d" % (s, a)], 64)
            for k, a in enumerate(sb + vb):
                out = pa[:, po + 64 * k:po + 64 * k + 64] if a in sb else pa[:, o + k - len(sb):o + 64 * nb:nb]
                act(out, T.etab[:], ["etab", t + "D", t + "B2"], ["pa%d.%d" % (s, a)], 64, bias=sc[:, 16 + a:17 + a], scale=sc[:, 8 + a:9 + a])
                pt.append("pa%d.%d" % (s, a))
            po = o + 64 * nb; vo += 64 * nb
        ts(T["pn%d" % s][:], pa[:], 1.0 / 16, 1280.0 - 15.0 / 32, A.mult, A.add, pt, ["pn%d" % s], 256)

    def slist(s, p):
        def mm():
            return [TE.matmul(T["Q%d" % p][:, c:128:4], T.qw[:, 128 * c:128 * c + 128], T["z%d" % p][:], True, True) for c in range(4)]
        add("T", 4 * 64 * PE, mm, QWT + ["z%d" % p], ["Q%d" % p], n=4)
        ts(T["ofs%d" % s][:], T["Q%d" % p][:, 0:128], CJ, None, A.add, None, ["Q%d" % p], ["ofs%d" % s], 128)

    def prep0():
        ctx[0] = ("prep", 0, 0, 0); r = []
        for k, nm in ((0, "lob"), (1, "hib")):
            for j, a in enumerate(SBL):
                ts(T.dg0[:, 32 * k + 16 * j:32 * k + 16 * j + 16], T.mk[:, 0:16], T.lob[:, 4 * k + a:4 * k + a + 1], None, A.mult, None, ["mk16", nm], ["dg0.%d%d" % (k, a)], 16)
                r.append("dg0.%d%d" % (k, a))
        add("T", 0.05, lambda: TE.matmul(T.KN1[:, 0:64], T.bos[:], T.dg0[:, 0:64], True, True), ["bosA", "bosB"] + r, ["KN1"])
        cp(T.vz0[:], T.KN1[:, 32:64], ["KN1"], ["vz0"], 32)
        tt(T.z0[:], T.KN1[:, 0:32], T.vz0[:], A.max, ["KN1", "vz0"], ["z0"], 32, 1.0)
        slist(2, 0)
        lists(0, 2, 0, ["lob", "hib"])

    def prep(p, l):
        ctx[0] = ("prep", p, l, 0); w = T["win%d" % p]; win = w[:, 0:128 * l]; sc = T["sc%d" % p]
        wt = ["w%d.%d.%s" % (p, k, x) for k in range(l) for x in ("own", "rem")]
        h = 8 * (l - 1); hh = 4 * (l - 1)
        um, us, vz, z = T["um%d" % p], T["us%d" % p], T["vz%d" % p], T["z%d" % p]
        tt(um[:], win.indirect(T.hl[:, h:h + 8]), T.mks[:], A.mult, wt + ["hl", "mks0", "mks1"], ["um%d" % p], 128, gather=True)
        scan(us[:], T.nst[:], um[:], 0.0, A.mult, A.add, ["nst", "um%d" % p], ["us%d" % p], 128)
        cp(vz[:], win.indirect(T.hs[:, hh + 2:hh + 4]), wt + ["hs"], ["vz%d" % p], 32, gather=True)
        tt(z[:], win.indirect(T.hs[:, hh:hh + 2]), vz[:], A.max, wt + ["hs", "vz%d" % p], ["z%d" % p], 32, gather=True)
        u, v = us[:, 15:64:16], us[:, 79:128:16]
        tt(sc[:, 0:4], u, v, A.min, ["us%d" % p], ["sc%d.lo" % p], 4)
        tt(sc[:, 4:8], u, v, A.max, ["us%d" % p], ["sc%d.hi" % p], 4)
        slist(p, p)
        lists(p, p, l, ["sc%d.lo" % p, "sc%d.hi" % p])

    def sets(p, l): return 2 if l == 0 else p

    def keys(p, l, u):
        sb, vb = CFG[p, l][0][u]
        return ["s%d.%d" % (a, i) for a in sb for i in range(16)] + ["v%s%d" % (k, h) for k in "dr" for h in range(len(vb))]

    def search(p, l, u):
        ctx[0] = ("search", p, l, u); s = sets(p, l); units = CFG[p, l][0]
        sb, vb = units[u]; nb = len(vb)
        po = sum(64 * len(a + b) for a, b in units[:u]); vo = sum(64 * len(b) for a, b in units[:u])
        K = T["K%d%d" % (p, u)]; kt = lambda x: "K%d%d.%s" % (p, u, x)
        x = T["x%d" % p]; w = 64 * (len(sb) + nb); ko = 64 * len(sb)
        grp = (p, l, u)
        kx = [kt(q) for q in keys(p, l, u)]
        add("T", w * PE, lambda: TE.matmul(K[:, 0:w], T.i64[:], T["pn%d" % s][:, po:po + w], True, False), ["i64", "pn%d" % s], kx + [kt("0")])
        for j, a in enumerate(sb):
            for i in range(16):
                r = 16 * SBL.index(a) + i
                o = T["as%d" % p][:, 64 * r:64 * r + 64]
                add("S", 0.065 + 64 * GE, lambda o=o, r=r, a=a, i=i: S.activation(o, T.yt[:].indirect(T["ofs%d" % s][:, 4 * r:4 * r + 4]), F.Abs, bias=x[:, 64 * l + 16 * a + i:64 * l + 16 * a + i + 1], scale=-1.0),
                    ["yt", "ofs%d" % s, xtok(p, l, a)], ["as%d.%d" % (p, r)])
                add("T", 64 * PE, lambda stop, o=o, j=j, i=i: TE.matmul(K[:, 64 * j:64 * j + 64], T.zs[:, 15 - i:143 - i], o, False, stop), ["zs", "as%d.%d" % (p, r), kt("0")], [kt("s%d.%d" % (a, i))], grp=grp)
        nc = 64 * 16 * nb // CH
        dv, rv = T["dv%d" % p], T["rv%d" % p]
        for h in range(nb):
            cs = range(h * nc // nb, (h + 1) * nc // nb)
            for c in cs:
                d = 16 * vo + CH * c
                tt(dv[:, d:d + CH], T.yt[:].indirect(T["ofv%d" % s][:, vo + CH // 16 * c:vo + CH // 16 * (c + 1)]), T["rep%d" % p][:, 2 * CH * l + CH * u:2 * CH * l + CH * u + CH], A.subtract,
                   ["yt"] + ["ofv%d.%d" % (s, a) for a in vb] + reptok[p, l, u], ["dv%d.%d" % (p, d)], CH, gather=True)
                if c % 2 == 1:
                    d -= CH; ctx[0] = ("relu", p, l, u)
                    ts(rv[:, d:d + 2 * CH], dv[:, d:d + 2 * CH], 0.0, None, A.max, None, ["dv%d.%d" % (p, d), "dv%d.%d" % (p, d + CH)], ["rv%d.%d" % (p, d)], 2 * CH, 0.5)
                    ctx[0] = ("search", p, l, u)
            d0 = 16 * vo + CH * cs[0]; d1 = 16 * vo + CH * (cs[-1] + 1)
            for kind, buf, z in (("d", dv, "zd"), ("r", rv, "zr")):
                toks = ["%sv%d.%d" % (kind, p, q) for q in range(d0, d1, CH if kind == "d" else 2 * CH)]
                def mm(stop, h=h, buf=buf, z=z, d0=d0, d1=d1):
                    return [TE.matmul(K[:, ko + 64 * h:ko + 64 * h + 64], T[z][:, 15 - i:143 - i], buf[:, d0 + i:d1:16], False, stop and i == 15) for i in range(16)]
                add("T", 16 * 64 * PE, mm, [z, kt("0")] + toks, [kt("v%s%d" % (kind, h))], n=16, grp=grp)

    def post(p, l, us):
        ctx[0] = ("post", p, l, us[0]); s = sets(p, l); units = CFG[p, l][0]
        ks, sc = T["ks%d" % p], T["sc%d" % s]; P = "%d" % p
        bl = []; kst = []
        for u in us:
            sb, vb = units[u]; K = T["K%d%d" % (p, u)]; ko = 64 * len(sb); nb = len(vb)
            kt = ["K%d%d.%s" % (p, u, q) for q in keys(p, l, u)]
            for j, a in enumerate(sb + vb):
                src = K[:, 64 * j:64 * j + 64] if a in sb else K[:, ko + j - len(sb):ko + 64 * nb:nb]
                scan(ks[:, 64 * a:64 * a + 64], T.seg[:], src, BIG, A.add, A.min, kt + ["seg"], ["ks%d.%d" % (p, a)], 64)
                kst.append("ks%d.%d" % (p, a)); bl.append(a)
        bl.sort(); c0, c1 = bl[0], bl[-1] + 1; n = c1 - c0; q = P + ".%d" % c0
        c = slice(c0, c1); wall = T.wall[:, 24 * p + 4 * l + c0:24 * p + 4 * l + c1]
        ts(T["ki" + P][:, c], ks[:, 64 * c0 + 63:64 * c1:64], 63.0, None, A.add, None, kst, ["ki" + q], 4)
        ts(T["ei" + P][:, c], T["ki" + P][:, c], 63, None, A.bitwise_and, None, ["ki" + q], ["ei" + q], 4)
        tt(T["tf" + P][:, c], T["ei" + P][:, c], sc[:, 8 + c0:8 + c1], A.mult, ["ei" + q, "sc%d.D" % s], ["tf" + q], 4)
        ctx[0] = ("win", p, l, us[0]); wt = "wall%d.%d.%d" % (p, l, c0)
        tt(wall, T["tf" + P][:, c], sc[:, 12 + c0:12 + c1], A.add, ["tf" + q, "sc%d.B1" % s], [wt], 4)
        ctx[0] = ("xup", p, l, us[0])
        cp(T["wo" + P][:, 2 * c0:2 * c0 + n], wall, [wt], ["wo" + q], 4)
        r0, r1 = 64 * l + 16 * c0, 64 * l + 16 * c1
        tt(T["dx" + P][:, 16 * c0:16 * c1], T.yt[:].indirect(T["wo" + P][:, 2 * c0:2 * c0 + n]), T["x" + P][:, r0:r1], A.subtract, ["yt", "wo" + q] + [xtok(p, l, a) for a in bl], ["dx" + q], 16 * n, gather=True)
        if p == 0:
            act(T.x1[:, r0:r1], T.dx0[:, 16 * c0:16 * c1], ["dx" + q], [xtok(1, l, a) for a in bl], 16 * n)
        else:
            act(T.xf[:, r0:r1], T.dx1[:, 16 * c0:16 * c1], ["dx" + q], ["xf.%d.%d" % (l, a) for a in bl], 16 * n)
        return wt

    def known(p, l, wts):
        ctx[0] = ("known", p, l, 0); P = "%d" % p; dg = T["dg%d" % (p + 1)]; w = T["win" + P]
        ts(T["wf" + P][:, 0:4], T.wall[:, 24 * p + 4 * l:24 * p + 4 * l + 4], -2048.0, 1.0 / 64, A.add, A.mult, wts, ["wf" + P], 4)
        tt(dg[:], T["wf" + P][:, 0:4].indirect(T.clist[:]), T.mk[:], A.mult, ["wf" + P, "clist", "mk16", "mk32", "mk"], ["dg%d" % (p + 1)], 64, gather=True)
        add("T", 64 * PE, lambda: TE.matmul(T["KN" + P][:, 0:64], T.bos[:], dg[:], True, True), ["bosA", "bosB", "dg%d" % (p + 1)], ["KN" + P])
        own = w[:, 128 * l:128 * l + 64]; ot = "w%d.%d.own" % (p, l)
        cp(own, T["KN" + P][:, 0:64], ["KN" + P], [ot], 64)
        dst = T.cores[(rank - 1) % len(T.cores)]
        rid, pid, _ = topo.addr(dst)
        m = topo.mask(core, dst)
        def send():
            G.remote_dma(w[:, 128 * l + 64:128 * l + 128], own, T.sem["arr%d_%d" % (p, l)], T.sem.snt, pid, rid, m)
        add("G", 1.0, send, [ot], ["w%d.%d.rem" % (p, l)], n=0, sem="arr%d_%d" % (p, l), val=len(topo.engines(core, dst)), lat=COST["REMOTE"])

    stores = [0]
    def store(out, in_, r):
        stores[0] += 1
        add("SY", 0.1, lambda: SY.dma_start(out, in_), r, [], sem="st", val=None, lat=2.0)

    prep0()
    allw = {0: [], 1: []}
    for k in range(2 * L):
        p, l = k % 2, k // 2
        units, posts = CFG[p, l]
        if p == 0:
            for u in range(len(units)): reps(0, l, u)
        if l: prep(p, l)
        for u in range(len(units)):
            if p == 1: reps(1, l, u)
            search(p, l, u)
        wts = [post(p, l, us) for us in posts]
        allw[p] += wts
        if l < L - 1: known(p, l, wts)
        else:
            cp(T.am[:, 24 * p:24 * p + 24], T.wall[:, 24 * p:24 * p + 24], allw[p], ["am%d" % p], 24)
            store(T.argm[:, 24 * p:24 * p + 24], T.am[:, 24 * p:24 * p + 24], ["am%d" % p])
        if p == 1 and l in (2, 4, 5):
            f = {2: 0, 4: 3, 5: 5}[l]
            store(T.xo[:, 64 * f:64 * l + 64], T.xf[:, 64 * f:64 * l + 64], ["xf.%d.%d" % (q, a) for q in range(f, l + 1) for a in range(4)])
    return ops, stores


def early(tag):
    k, p = tag[0], tag[1]; v = 0.0
    if k in ("prep", "post", "win", "known"): v += PRI["chain"]
    if k in ("xup", "reps"): v += PRI["xup"]
    if k == "relu": v += PRI["relu"]
    if k != "setup": v += PRI["p1"] * p
    return v


def plan(ops):
    n = len(ops); WAKE = COST["WAKE"]
    succ = [[] for _ in range(n)]
    for i, o in enumerate(ops):
        for d in o["deps"]: succ[d].append(i)
    way = [0.0] * n
    for i in range(n - 1, -1, -1):
        o = ops[i]
        way[i] = o["dur"] + max([o["lat"] + WAKE + way[j] for j in succ[i]] + [0.0])
    pri = [way[i] + early(ops[i]["tag"]) for i in range(n)]
    left = [len(o["deps"]) for o in ops]
    ready = [0.0] * n
    free = {"V": 0.0, "S": 0.0, "G": 0.0, "T": 0.0, "SY": 0.0}
    cand = {q: [] for q in free}
    for i in range(n):
        if left[i] == 0: cand[ops[i]["q"]].append(i)
    order, start = [], [0.0] * n
    while len(order) < n:
        best = None
        for q in cand:
            for i in cand[q]:
                key = (max(free[q], ready[i]), -pri[i], i)
                if best is None or key < best: best = key
        t, i = best[0], best[2]
        o = ops[i]; q = o["q"]
        cand[q].remove(i)
        start[i] = t; fin = t + o["dur"]; free[q] = fin
        order.append(i)
        for j in succ[i]:
            same = ops[j]["q"] == q and q == "T"
            ready[j] = max(ready[j], t if same else fin + o["lat"] + WAKE)
            left[j] -= 1
            if left[j] == 0: cand[ops[j]["q"]].append(j)
    pos = {i: k for k, i in enumerate(order)}
    order.sort(key=lambda i: (start[i], pos[i]))
    return order


CACHE = {}


def rank_program(g, core, T, topo):
    rank = T.rank_of(core)
    if rank is None:
        return
    ops, stores = build(g, core, T, topo, rank)
    if "order" not in CACHE: CACHE["order"] = plan(ops)
    order = CACHE["order"]
    eng = {"V": g.vector, "S": g.scalar, "G": g, "T": g.tensor, "SY": g.sync}
    csem = {"V": T.sem.cV, "S": T.sem.cS, "T": T.sem.cT, "G": T.sem.cG}
    count = {q: 0 for q in csem}
    done = {}
    seen = {q: {} for q in eng}
    last = {ops[i]["grp"]: i for i in order if ops[i]["grp"]}
    for i in order:
        o = ops[i]; q = o["q"]; need = {}
        for d in o["deps"]:
            if ops[d]["q"] == q and q == "T": continue
            nm, v = done[d]
            need[nm] = max(need.get(nm, 0), v)
        for nm in sorted(need):
            if seen[q].get(nm, 0) < need[nm]:
                eng[q].wait_ge(T.sem[nm], need[nm]); seen[q][nm] = need[nm]
        res = o["fn"](last[o["grp"]] == i) if o["grp"] else o["fn"]()
        if o["sem"] is not None:
            if q != "G": res.then_inc(T.sem[o["sem"]], 16)
            done[i] = (o["sem"], o["val"])
        else:
            for x in (res if o["n"] > 1 else [res]): x.then_inc(csem[q], 1)
            count[q] += o["n"]
            done[i] = ("c" + q, count[q])
    g.sync.wait_ge(T.sem.st, 16 * stores[0])
    dst = T.cores[(rank - 1) % len(T.cores)]
    g.wait_ge(T.sem.snt, 2 * (L - 1) * len(topo.engines(core, dst)))
    for q in ("V", "S", "T", "G"):
        g.sync.wait_ge(csem[q], count[q])
